import numpy as np
import ml_dtypes


def mxq(x, axis, fmt="e4m3"):
    dtype, down = {"e4m3": (ml_dtypes.float8_e4m3fn, 7), "e5m2": (ml_dtypes.float8_e5m2, 14)}[fmt]
    v = np.moveaxis(np.asarray(x, np.float32).astype(ml_dtypes.bfloat16).astype(np.float64), axis, -1)
    blocks = v.reshape(v.shape[:-1] + (-1, 32))
    amax = np.abs(blocks).max(-1, keepdims=True)
    byte = np.maximum(np.where(amax > 0, np.frexp(amax)[1] - 1 + 127, 0) - down, 1)
    scale = np.exp2(byte - 127.0)
    codes = (blocks / scale).astype(np.float32).astype(dtype).astype(np.float64)
    return np.moveaxis((codes * scale).reshape(v.shape), -1, axis)


WIDE = False


def mx_kscale(k):
    if not WIDE:
        return np.ones(k)
    levels = np.array([10, -10, 5, -5, 0])
    if k % 512:
        return np.exp2(np.random.permutation(np.resize(levels, k // 32))).repeat(32)
    a = np.empty((k // 512, 16))
    for p in range(k // 512):
        a[p, :8] = np.random.permutation(np.resize(levels, 8))
        for g in range(8):
            far = levels[np.abs(levels - a[p, g]) >= 10]
            a[p, g + 8] = far[np.random.randint(len(far))]
    return np.exp2(a.ravel()).repeat(32)


def f64(x):
    return np.asarray(x).astype(np.float64)


def striped(idx):
    return np.tile(idx.reshape(-1, 16).T, (8, 1)).astype(np.uint16)


def unstriped(offs):
    return offs[:16].T.reshape(-1).astype(np.int64)


E2M1 = np.array([0.0, 0.5, 1.0, 1.5, 2.0, 3.0, 4.0, 6.0, -0.0, -0.5, -1.0, -1.5, -2.0, -3.0, -4.0, -6.0])


def pack_fp4(w):
    k, n = w.shape
    w = f64(np.asarray(w, np.float32).astype(ml_dtypes.bfloat16)).reshape(k // 32, 32, n)
    amax = np.abs(w).max(1)
    mant, ex = np.frexp(amax / 6.0)
    byte = np.clip(np.where(amax > 0, np.where(mant > 0.5, ex, ex - 1) + 127, 1), 1, 254)
    scaled = (w * np.exp2(127.0 - byte)[:, None, :]).reshape(k, n).astype(np.float32)
    c = np.ascontiguousarray(scaled.reshape(k // 512, 128, 4, n).transpose(0, 1, 3, 2)).astype(ml_dtypes.float4_e2m1fn).view(np.uint8) & 0xF
    words = (c[..., 0::2] | (c[..., 1::2] << 4)).reshape(k // 512, 128, 2 * n)
    return np.ascontiguousarray(words), np.ascontiguousarray(byte.astype(np.uint8).reshape(k // 512, 16, n))


def unpack_fp4(words, scales):
    g, _, n = scales.shape
    words = np.ascontiguousarray(words).reshape(g, 128, n, 2)
    nib = np.empty((g, 128, n, 4), np.uint8)
    nib[..., 0::2] = words & 0xF
    nib[..., 1::2] = words >> 4
    vals = E2M1[nib] * np.repeat(np.exp2(scales.astype(np.float64) - 127.0), 8, axis=1)[..., None]
    return vals.transpose(0, 1, 3, 2).reshape(g * 512, n)


def relu(v):
    return np.maximum(v, 0.0)


def sigmoid(v):
    return 1.0 / (1.0 + np.exp(-np.maximum(v, -700.0)))


K, T, N, U = 1024, 512, 128, 1024


def setup_inputs():
    n = np.random.standard_normal
    s = mx_kscale(K)[:, None]
    packed_xT = pack_fp4(n((K, T)) * s)
    return {
        "x_words": packed_xT[0],
        "x_scales": packed_xT[1],
        "mem": n((N, U)).astype(np.float32),
        "w1": (n((K, N)) / np.sqrt(K) / s).astype(np.float32),
        "w2": (n((K, N)) / np.sqrt(K) / s).astype(np.float32),
        "slot": striped(np.random.permutation(U)[:T]),
    }


def reference(x_words, x_scales, mem, w1, w2, slot):
    old = f64(mem)[:, unstriped(slot)]
    xq = unpack_fp4(x_words, x_scales)
    g = sigmoid(mxq(f64(w2), 0, "e4m3").T @ xq)
    y = relu(mxq(f64(w1), 0, "e4m3").T @ xq)
    out = f64(mem).copy()
    out[:, unstriped(slot)] = old + g * (y - old)
    return out

@@ -1,0 +1,106 @@
+from contextlib import ExitStack
+
+import concourse.mybir as mybir
+
+K, T, N, U = 1024, 512, 128, 1024
+FLOPS = 2 * 2 * K * T * N
+
+F32 = mybir.dt.float32
+BF16 = mybir.dt.bfloat16
+I32 = mybir.dt.int32
+U32 = mybir.dt.uint32
+U16 = mybir.dt.uint16
+U8 = mybir.dt.uint8
+FP8X4 = mybir.dt.float8_e4m3fn_x4
+FP4X4 = mybir.dt.float4_e2m1fn_x4
+ALU = mybir.AluOpType
+ACT = mybir.ActivationFunctionType
+
+P = 128
+PACK = 4
+PASSES = K // (P * PACK)
+PIECE = 128
+PIECES = T // PIECE
+
+
+def tile_picked_wgmem_relu_l_kernel(tc, x_words, x_scales, mem, w1, w2, slot, out):
+    nc = tc.nc
+    with ExitStack() as ctx:
+        sb = ctx.enter_context(tc.tile_pool(name="sb", bufs=1))
+        ps = ctx.enter_context(tc.psum_pool(name="ps", bufs=1))
+
+        offsets = sb.tile([P, T // 16], U16, name="offsets")
+        window = sb.tile([P, U], F32, name="window")
+        xw = sb.tile([P, PASSES * 2 * T], U8, name="xw", align_bytes=64)
+        xs = sb.tile([P, PASSES * T], U8, name="xs", align_bytes=64)
+        w1raw = sb.tile([P, PASSES, PACK, N], F32, name="w1raw")
+        w2raw = [sb.tile([P, PACK, N], F32, name="w2raw%d" % z) for z in range(PASSES)]
+
+        nc.vector.memset(xs[:].bitcast(I32), 0)
+
+        nc.sync.dma_start(out=w1raw[:].rearrange("p z j m -> p z (j m)"), in_=w1.rearrange("(z p j) m -> p z (j m)", z=PASSES, j=PACK))
+        for q in range(4):
+            eng = nc.scalar if q < 2 else nc.gpsimd
+            eng.dma_start(
+                out=xs[32 * q : 32 * q + 4, :].bitcast(I32).rearrange("r (z c) -> r z c", z=PASSES),
+                in_=x_scales[:, 4 * q : 4 * q + 4, :].bitcast(I32).rearrange("z r c -> r z c"),
+            )
+        nc.sync.dma_start(out=xw[:].bitcast(I32).rearrange("p (z c) -> p z c", z=PASSES), in_=x_words.bitcast(I32).rearrange("z p c -> p z c"))
+        nc.sync.dma_start(offsets[:], slot)
+        nc.sync.dma_start(out=window[:], in_=mem)
+        for z in range(PASSES):
+            nc.sync.dma_start(out=w2raw[z][:].rearrange("p j m -> p (j m)"), in_=w2[z * P * PACK : (z + 1) * P * PACK, :].rearrange("(p j) m -> p (j m)", j=PACK))
+
+        def quantise(raw, name, vector_cols):
+            grouped = sb.tile([P, N, PACK], BF16, name=name + "g", align_bytes=64)
+            codes = sb.tile([P, N], U32, name=name + "c", align_bytes=64)
+            scales = sb.tile([P, N], U8, name=name + "s", align_bytes=64)
+            src = raw.rearrange("p j m -> p m j")
+            if vector_cols > 0:
+                nc.vector.tensor_copy(out=grouped[:, :vector_cols, :], in_=src[:, :vector_cols, :])
+            if vector_cols < N:
+                nc.scalar.copy(out=grouped[:, vector_cols:, :], in_=src[:, vector_cols:, :])
+            nc.vector.quantize_mx(out=codes[:].bitcast(FP8X4), scales=scales[:], in_=grouped[:].rearrange("p m j -> p (m j)"))
+            return codes, scales
+
+        def product(acc, q, z, c0, width):
+            nc.tensor.matmul_mx(
+                out=acc,
+                lhsT=q[0][:].bitcast(FP8X4),
+                lhsT_scale=q[1][:],
+                rhs=xw[:, 2 * (z * T + c0) : 2 * (z * T + c0 + width)].bitcast(FP4X4),
+                rhs_scale=xs[:, z * T + c0 : z * T + c0 + width],
+                start=(z == 0),
+                stop=(z == PASSES - 1),
+            )
+
+        warm = sb.tile([P, 1], F32, name="warm")
+        nc.vector.memset(warm[:], 0.0)
+        warm2 = sb.tile([P, 1], F32, name="warm2")
+        nc.scalar.activation(out=warm2[:], in_=warm[:], func=ACT.Sigmoid)
+
+        q1 = [quantise(w1raw[:, 0], "w1a", N), quantise(w1raw[:, 1], "w1b", 0)]
+        yacc = ps.tile([P, T], F32, name="yacc")
+        for z in range(PASSES):
+            product(yacc[:], q1[z], z, 0, T)
+
+        old = sb.tile([P, T], F32, name="old")
+        nc.vector.tensor_copy(old[:], window[:].indirect(offsets[:]))
+
+        q2 = [quantise(w2raw[0][:], "w2a", 0), quantise(w2raw[1][:], "w2b", 80)]
+
+        diff = sb.tile([P, T], F32, name="diff")
+        nc.vector.scalar_tensor_tensor(out=diff[:], in0=yacc[:], scalar=0.0, in1=old[:], op0=ALU.max, op1=ALU.subtract)
+
+        for i in range(PIECES):
+            cols = slice(i * PIECE, (i + 1) * PIECE)
+            gacc = ps.tile([P, PIECE], F32, name="gacc%d" % i)
+            for z in range(PASSES):
+                product(gacc[:], q2[z], z, i * PIECE, PIECE)
+            gate = sb.tile([P, PIECE], F32, name="gate%d" % i)
+            nc.scalar.activation(out=gate[:], in_=gacc[:], func=ACT.Sigmoid)
+            step = sb.tile([P, PIECE], F32, name="step%d" % i)
+            nc.vector.tensor_tensor(step[:], diff[:, cols], gate[:], ALU.mult)
+            nc.vector.tensor_tensor(window[:].indirect(offsets[:, i * PIECE // 16 : (i + 1) * PIECE // 16]), step[:], old[:, cols], ALU.add)
+
+        nc.sync.dma_start(out=out, in_=window[:])

@@ -33,26 +33,44 @@ def tile_picked_wgmem_relu_l_kernel(tc, x_words, x_scales, mem, w1, w2, slot, ou
         window = sb.tile([P, U], F32, name="window")
         xw = sb.tile([P, PASSES * 2 * T], U8, name="xw", align_bytes=64)
         xs = sb.tile([P, PASSES * T], U8, name="xs", align_bytes=64)
-        w1raw = sb.tile([P, PASSES, PACK, N], F32, name="w1raw")
+        w1raw = [sb.tile([P, PACK, N], F32, name="w1raw%d" % z) for z in range(PASSES)]
         w2raw = [sb.tile([P, PACK, N], F32, name="w2raw%d" % z) for z in range(PASSES)]
 
-        nc.vector.memset(xs[:].bitcast(I32), 0)
-
-        nc.sync.dma_start(out=w1raw[:].rearrange("p z j m -> p z (j m)"), in_=w1.rearrange("(z p j) m -> p z (j m)", z=PASSES, j=PACK))
-        for q in range(4):
-            eng = nc.scalar if q < 2 else nc.gpsimd
+        def sc(eng, q):
             eng.dma_start(
                 out=xs[32 * q : 32 * q + 4, :].bitcast(I32).rearrange("r (z c) -> r z c", z=PASSES),
                 in_=x_scales[:, 4 * q : 4 * q + 4, :].bitcast(I32).rearrange("z r c -> r z c"),
             )
-        nc.sync.dma_start(out=xw[:].bitcast(I32).rearrange("p (z c) -> p z c", z=PASSES), in_=x_words.bitcast(I32).rearrange("z p c -> p z c"))
-        nc.sync.dma_start(offsets[:], slot)
-        nc.sync.dma_start(out=window[:], in_=mem)
-        for z in range(PASSES):
+
+        def lw1(z):
+            nc.sync.dma_start(out=w1raw[z][:].rearrange("p j m -> p (j m)"), in_=w1[z * P * PACK : (z + 1) * P * PACK, :].rearrange("(p j) m -> p (j m)", j=PACK))
+
+        def lx():
+            nc.sync.dma_start(out=xw[:].bitcast(I32).rearrange("p (z c) -> p z c", z=PASSES), in_=x_words.bitcast(I32).rearrange("z p c -> p z c"))
+
+        def lslot():
+            nc.sync.dma_start(offsets[:], slot)
+
+        def lmem():
+            nc.sync.dma_start(out=window[:], in_=mem)
+
+        def lw2(z):
             nc.sync.dma_start(out=w2raw[z][:].rearrange("p j m -> p (j m)"), in_=w2[z * P * PACK : (z + 1) * P * PACK, :].rearrange("(p j) m -> p (j m)", j=PACK))
 
-        def quantise(raw, name, vector_cols):
-            grouped = sb.tile([P, N, PACK], BF16, name=name + "g", align_bytes=64)
+        lw2(0)
+        sc(nc.sync, 0)
+        sc(nc.sync, 1)
+        sc(nc.sync, 2)
+        sc(nc.sync, 3)
+        lx()
+        lw2(1)
+        lw1(0)
+        lw1(1)
+        lmem()
+        lslot()
+
+        def quantise(raw, name, vector_cols, tag):
+            grouped = sb.tile([P, N, PACK], BF16, name=name + "g", tag=tag, align_bytes=64)
             codes = sb.tile([P, N], U32, name=name + "c", align_bytes=64)
             scales = sb.tile([P, N], U8, name=name + "s", align_bytes=64)
             src = raw.rearrange("p j m -> p m j")
@@ -79,28 +97,22 @@ def tile_picked_wgmem_relu_l_kernel(tc, x_words, x_scales, mem, w1, w2, slot, ou
         warm2 = sb.tile([P, 1], F32, name="warm2")
         nc.scalar.activation(out=warm2[:], in_=warm[:], func=ACT.Sigmoid)
 
-        q1 = [quantise(w1raw[:, 0], "w1a", N), quantise(w1raw[:, 1], "w1b", 0)]
+        q2 = [quantise(w2raw[0][:], "w2a", 80, "g2"), quantise(w2raw[1][:], "w2b", 80, "g3")]
+        gacc = ps.tile([P, T], F32, name="gacc")
+        for z in range(PASSES):
+            product(gacc[:], q2[z], z, 0, T)
+        q1 = [quantise(w1raw[0][:], "w1a", 0, "g0"), quantise(w1raw[1][:], "w1b", 128, "g1")]
         yacc = ps.tile([P, T], F32, name="yacc")
         for z in range(PASSES):
             product(yacc[:], q1[z], z, 0, T)
-
-        old = sb.tile([P, T], F32, name="old")
-        nc.vector.tensor_copy(old[:], window[:].indirect(offsets[:]))
-
-        q2 = [quantise(w2raw[0][:], "w2a", 0), quantise(w2raw[1][:], "w2b", 80)]
-
-        diff = sb.tile([P, T], F32, name="diff")
-        nc.vector.scalar_tensor_tensor(out=diff[:], in0=yacc[:], scalar=0.0, in1=old[:], op0=ALU.max, op1=ALU.subtract)
-
-        for i in range(PIECES):
-            cols = slice(i * PIECE, (i + 1) * PIECE)
-            gacc = ps.tile([P, PIECE], F32, name="gacc%d" % i)
-            for z in range(PASSES):
-                product(gacc[:], q2[z], z, i * PIECE, PIECE)
-            gate = sb.tile([P, PIECE], F32, name="gate%d" % i)
-            nc.scalar.activation(out=gate[:], in_=gacc[:], func=ACT.Sigmoid)
-            step = sb.tile([P, PIECE], F32, name="step%d" % i)
-            nc.vector.tensor_tensor(step[:], diff[:, cols], gate[:], ALU.mult)
-            nc.vector.tensor_tensor(window[:].indirect(offsets[:, i * PIECE // 16 : (i + 1) * PIECE // 16]), step[:], old[:, cols], ALU.add)
+        keep = sb.tile([P, T], F32, name="keep")
+        gate = sb.tile([P, T], F32, name="gate")
+        nc.scalar.activation(out=keep[:], in_=gacc[:], func=ACT.Sigmoid, scale=-1.0)
+        nc.scalar.activation(out=gate[:], in_=gacc[:], func=ACT.Sigmoid)
+        kept = sb.tile([P, T], F32, name="kept")
+        nc.vector.tensor_tensor(kept[:], window[:].indirect(offsets[:]), keep[:], ALU.mult)
+        fresh = sb.tile([P, T], F32, name="fresh")
+        nc.vector.scalar_tensor_tensor(out=fresh[:], in0=yacc[:], scalar=0.0, in1=gate[:], op0=ALU.max, op1=ALU.mult)
+        nc.vector.tensor_tensor(window[:].indirect(offsets[:]), kept[:], fresh[:], ALU.add)
 
         nc.sync.dma_start(out=out, in_=window[:])

@@ -92,26 +92,24 @@ def tile_picked_wgmem_relu_l_kernel(tc, x_words, x_scales, mem, w1, w2, slot, ou
                 stop=(z == PASSES - 1),
             )
 
-        warm = sb.tile([P, 1], F32, name="warm")
-        nc.vector.memset(warm[:], 0.0)
-        warm2 = sb.tile([P, 1], F32, name="warm2")
-        nc.scalar.activation(out=warm2[:], in_=warm[:], func=ACT.Sigmoid)
-
-        q2 = [quantise(w2raw[0][:], "w2a", 80, "g2"), quantise(w2raw[1][:], "w2b", 80, "g3")]
+        q2 = [quantise(w2raw[0][:], "w2a", 128, "g2"), quantise(w2raw[1][:], "w2b", 128, "g3")]
         gacc = ps.tile([P, T], F32, name="gacc")
         for z in range(PASSES):
             product(gacc[:], q2[z], z, 0, T)
-        q1 = [quantise(w1raw[0][:], "w1a", 0, "g0"), quantise(w1raw[1][:], "w1b", 128, "g1")]
+        q1 = [quantise(w1raw[0][:], "w1a", 128, "g0"), quantise(w1raw[1][:], "w1b", 128, "g1")]
         yacc = ps.tile([P, T], F32, name="yacc")
         for z in range(PASSES):
             product(yacc[:], q1[z], z, 0, T)
-        keep = sb.tile([P, T], F32, name="keep")
+        half = T // 2
+        keep = [sb.tile([P, half], F32, name="keep%d" % h, tag="keep%d" % h) for h in range(2)]
         gate = sb.tile([P, T], F32, name="gate")
-        nc.scalar.activation(out=keep[:], in_=gacc[:], func=ACT.Sigmoid, scale=-1.0)
-        nc.scalar.activation(out=gate[:], in_=gacc[:], func=ACT.Sigmoid)
         kept = sb.tile([P, T], F32, name="kept")
-        nc.vector.tensor_tensor(kept[:], window[:].indirect(offsets[:]), keep[:], ALU.mult)
-        fresh = sb.tile([P, T], F32, name="fresh")
+        for h in range(2):
+            nc.scalar.activation(out=keep[h][:], in_=gacc[:, h * half : (h + 1) * half], func=ACT.Sigmoid, scale=-1.0)
+        nc.scalar.activation(out=gate[:], in_=gacc[:], func=ACT.Sigmoid)
+        for h in range(2):
+            nc.vector.tensor_tensor(kept[:, h * half : (h + 1) * half], window[:].indirect(offsets[:, h * half // 16 : (h + 1) * half // 16]), keep[h][:], ALU.mult)
+        fresh = sb.tile([P, T], F32, name="fresh", tag="keep0")
         nc.vector.scalar_tensor_tensor(out=fresh[:], in0=yacc[:], scalar=0.0, in1=gate[:], op0=ALU.max, op1=ALU.mult)
         nc.vector.tensor_tensor(window[:].indirect(offsets[:]), kept[:], fresh[:], ALU.add)
 

@@ -58,16 +58,16 @@ def tile_picked_wgmem_relu_l_kernel(tc, x_words, x_scales, mem, w1, w2, slot, ou
             nc.sync.dma_start(out=w2raw[z][:].rearrange("p j m -> p (j m)"), in_=w2[z * P * PACK : (z + 1) * P * PACK, :].rearrange("(p j) m -> p (j m)", j=PACK))
 
         lw2(0)
+        lw2(1)
         sc(nc.sync, 0)
         sc(nc.sync, 1)
         sc(nc.sync, 2)
         sc(nc.sync, 3)
         lx()
-        lw2(1)
         lw1(0)
         lw1(1)
-        lmem()
         lslot()
+        lmem()
 
         def quantise(raw, name, vector_cols, tag):
             grouped = sb.tile([P, N, PACK], BF16, name=name + "g", tag=tag, align_bytes=64)

@@ -19,8 +19,8 @@ ACT = mybir.ActivationFunctionType
 P = 128
 PACK = 4
 PASSES = K // (P * PACK)
-PIECE = 128
-PIECES = T // PIECE
+FIRST = 128
+SHARED = 256
 
 
 def tile_picked_wgmem_relu_l_kernel(tc, x_words, x_scales, mem, w1, w2, slot, out):
@@ -36,81 +36,82 @@ def tile_picked_wgmem_relu_l_kernel(tc, x_words, x_scales, mem, w1, w2, slot, ou
         w1raw = [sb.tile([P, PACK, N], F32, name="w1raw%d" % z) for z in range(PASSES)]
         w2raw = [sb.tile([P, PACK, N], F32, name="w2raw%d" % z) for z in range(PASSES)]
 
-        def sc(eng, q):
-            eng.dma_start(
+        def load_weight(raw, w, z):
+            nc.sync.dma_start(out=raw[z][:].rearrange("p j m -> p (j m)"), in_=w[z * P * PACK : (z + 1) * P * PACK, :].rearrange("(p j) m -> p (j m)", j=PACK))
+
+        for z in range(PASSES):
+            load_weight(w2raw, w2, z)
+        for q in range(4):
+            nc.sync.dma_start(
                 out=xs[32 * q : 32 * q + 4, :].bitcast(I32).rearrange("r (z c) -> r z c", z=PASSES),
                 in_=x_scales[:, 4 * q : 4 * q + 4, :].bitcast(I32).rearrange("z r c -> r z c"),
             )
+        nc.sync.dma_start(out=xw[:].bitcast(I32).rearrange("p (z c) -> p z c", z=PASSES), in_=x_words.bitcast(I32).rearrange("z p c -> p z c"))
+        for z in range(PASSES):
+            load_weight(w1raw, w1, z)
+        nc.sync.dma_start(offsets[:], slot)
+        nc.sync.dma_start(out=window[:], in_=mem)
 
-        def lw1(z):
-            nc.sync.dma_start(out=w1raw[z][:].rearrange("p j m -> p (j m)"), in_=w1[z * P * PACK : (z + 1) * P * PACK, :].rearrange("(p j) m -> p (j m)", j=PACK))
-
-        def lx():
-            nc.sync.dma_start(out=xw[:].bitcast(I32).rearrange("p (z c) -> p z c", z=PASSES), in_=x_words.bitcast(I32).rearrange("z p c -> p z c"))
-
-        def lslot():
-            nc.sync.dma_start(offsets[:], slot)
-
-        def lmem():
-            nc.sync.dma_start(out=window[:], in_=mem)
-
-        def lw2(z):
-            nc.sync.dma_start(out=w2raw[z][:].rearrange("p j m -> p (j m)"), in_=w2[z * P * PACK : (z + 1) * P * PACK, :].rearrange("(p j) m -> p (j m)", j=PACK))
-
-        lw2(0)
-        lw2(1)
-        sc(nc.sync, 0)
-        sc(nc.sync, 1)
-        sc(nc.sync, 2)
-        sc(nc.sync, 3)
-        lx()
-        lw1(0)
-        lw1(1)
-        lslot()
-        lmem()
-
-        def quantise(raw, name, vector_cols, tag):
-            grouped = sb.tile([P, N, PACK], BF16, name=name + "g", tag=tag, align_bytes=64)
+        def quantise(raw, name):
+            grouped = sb.tile([P, N, PACK], BF16, name=name + "g", align_bytes=64)
             codes = sb.tile([P, N], U32, name=name + "c", align_bytes=64)
             scales = sb.tile([P, N], U8, name=name + "s", align_bytes=64)
-            src = raw.rearrange("p j m -> p m j")
-            if vector_cols > 0:
-                nc.vector.tensor_copy(out=grouped[:, :vector_cols, :], in_=src[:, :vector_cols, :])
-            if vector_cols < N:
-                nc.scalar.copy(out=grouped[:, vector_cols:, :], in_=src[:, vector_cols:, :])
+            nc.vector.tensor_copy(out=grouped[:], in_=raw.rearrange("p j m -> p m j"))
             nc.vector.quantize_mx(out=codes[:].bitcast(FP8X4), scales=scales[:], in_=grouped[:].rearrange("p m j -> p (m j)"))
             return codes, scales
 
-        def product(acc, q, z, c0, width):
+        def product(acc, q, z, lo, hi):
             nc.tensor.matmul_mx(
-                out=acc,
+                out=acc[:],
                 lhsT=q[0][:].bitcast(FP8X4),
                 lhsT_scale=q[1][:],
-                rhs=xw[:, 2 * (z * T + c0) : 2 * (z * T + c0 + width)].bitcast(FP4X4),
-                rhs_scale=xs[:, z * T + c0 : z * T + c0 + width],
+                rhs=xw[:, 2 * (z * T + lo) : 2 * (z * T + hi)].bitcast(FP4X4),
+                rhs_scale=xs[:, z * T + lo : z * T + hi],
                 start=(z == 0),
                 stop=(z == PASSES - 1),
             )
 
-        q2 = [quantise(w2raw[0][:], "w2a", 128, "g2"), quantise(w2raw[1][:], "w2b", 128, "g3")]
-        gacc = ps.tile([P, T], F32, name="gacc")
-        for z in range(PASSES):
-            product(gacc[:], q2[z], z, 0, T)
-        q1 = [quantise(w1raw[0][:], "w1a", 128, "g0"), quantise(w1raw[1][:], "w1b", 128, "g1")]
-        yacc = ps.tile([P, T], F32, name="yacc")
-        for z in range(PASSES):
-            product(yacc[:], q1[z], z, 0, T)
-        half = T // 2
-        keep = [sb.tile([P, half], F32, name="keep%d" % h, tag="keep%d" % h) for h in range(2)]
+        def slots(lo, hi):
+            return window[:].indirect(offsets[:, lo // 16 : hi // 16])
+
+        pieces = ((0, FIRST), (FIRST, SHARED), (SHARED, T))
         gate = sb.tile([P, T], F32, name="gate")
         kept = sb.tile([P, T], F32, name="kept")
-        for h in range(2):
-            nc.scalar.activation(out=keep[h][:], in_=gacc[:, h * half : (h + 1) * half], func=ACT.Sigmoid, scale=-1.0)
-        nc.scalar.activation(out=gate[:], in_=gacc[:], func=ACT.Sigmoid)
-        for h in range(2):
-            nc.vector.tensor_tensor(kept[:, h * half : (h + 1) * half], window[:].indirect(offsets[:, h * half // 16 : (h + 1) * half // 16]), keep[h][:], ALU.mult)
-        fresh = sb.tile([P, T], F32, name="fresh", tag="keep0")
-        nc.vector.scalar_tensor_tensor(out=fresh[:], in0=yacc[:], scalar=0.0, in1=gate[:], op0=ALU.max, op1=ALU.mult)
-        nc.vector.tensor_tensor(window[:].indirect(offsets[:]), kept[:], fresh[:], ALU.add)
+        fresh = sb.tile([P, T], F32, name="fresh")
+        old = sb.tile([P, T - SHARED], F32, name="old")
+        new = sb.tile([P, FIRST], F32, name="new")
+        keep_late = sb.tile([P, T - SHARED], F32, name="keep_late")
+        keep = (fresh[:, 0:SHARED], keep_late[:])
+        kept_first = kept[:, SHARED : SHARED + FIRST]
+        fresh_at = (fresh[:, SHARED : SHARED + FIRST], fresh[:, FIRST:SHARED], fresh[:, SHARED:T])
+
+        q2 = [quantise(w2raw[z][:], "w2_%d" % z) for z in range(PASSES)]
+        for h, (lo, hi) in enumerate(((0, SHARED), (SHARED, T))):
+            gacc = ps.tile([P, hi - lo], F32, name="gacc%d" % lo)
+            for z in range(PASSES):
+                product(gacc, q2[z], z, lo, hi)
+            nc.scalar.activation(out=keep[h], in_=gacc[:], func=ACT.Sigmoid, scale=-1.0)
+            nc.scalar.activation(out=gate[:, lo:hi], in_=gacc[:], func=ACT.Sigmoid)
+
+        yacc = [ps.tile([P, hi - lo], F32, name="yacc%d" % lo) for lo, hi in pieces]
+        for z in range(PASSES):
+            q1 = quantise(w1raw[z][:], "w1_%d" % z)
+            for acc, (lo, hi) in zip(yacc, pieces):
+                product(acc, q1, z, lo, hi)
+
+        def make_fresh(i):
+            lo, hi = pieces[i]
+            nc.vector.scalar_tensor_tensor(out=fresh_at[i], in0=yacc[i][:], scalar=0.0, in1=gate[:, lo:hi], op0=ALU.max, op1=ALU.mult)
+
+        nc.scalar.activation(out=old[:], in_=slots(SHARED, T), func=ACT.Copy)
+        nc.vector.tensor_tensor(kept_first, slots(0, FIRST), fresh[:, 0:FIRST], ALU.mult)
+        make_fresh(0)
+        nc.vector.tensor_tensor(kept[:, FIRST:SHARED], slots(FIRST, SHARED), fresh[:, FIRST:SHARED], ALU.mult)
+        nc.vector.tensor_tensor(new[:], kept_first, fresh_at[0], ALU.add)
+        nc.scalar.activation(out=slots(0, FIRST), in_=new[:], func=ACT.Copy)
+        make_fresh(1)
+        make_fresh(2)
+        nc.vector.tensor_tensor(kept[:, SHARED:T], old[:], keep_late[:], ALU.mult)
+        nc.vector.tensor_tensor(slots(FIRST, T), kept[:, FIRST:T], fresh[:, FIRST:T], ALU.add)
 
         nc.sync.dma_start(out=out, in_=window[:])

@@ -19,7 +19,6 @@ ACT = mybir.ActivationFunctionType
 P = 128
 PACK = 4
 PASSES = K // (P * PACK)
-FIRST = 128
 SHARED = 256
 
 
@@ -74,24 +73,26 @@ def tile_picked_wgmem_relu_l_kernel(tc, x_words, x_scales, mem, w1, w2, slot, ou
         def slots(lo, hi):
             return window[:].indirect(offsets[:, lo // 16 : hi // 16])
 
-        pieces = ((0, FIRST), (FIRST, SHARED), (SHARED, T))
-        gate = sb.tile([P, T], F32, name="gate")
+        pieces = ((0, SHARED), (SHARED, T))
         kept = sb.tile([P, T], F32, name="kept")
         fresh = sb.tile([P, T], F32, name="fresh")
         old = sb.tile([P, T - SHARED], F32, name="old")
-        new = sb.tile([P, FIRST], F32, name="new")
-        keep_late = sb.tile([P, T - SHARED], F32, name="keep_late")
-        keep = (fresh[:, 0:SHARED], keep_late[:])
-        kept_first = kept[:, SHARED : SHARED + FIRST]
-        fresh_at = (fresh[:, SHARED : SHARED + FIRST], fresh[:, FIRST:SHARED], fresh[:, SHARED:T])
+        gate_second = sb.tile([P, T - SHARED], F32, name="gate_second")
+        keep_second = sb.tile([P, T - SHARED], F32, name="keep_second")
+        gate = (kept[:, SHARED:T], gate_second[:])
+        quarter = SHARED // 2
+        keep_first = fresh[:].rearrange("p (h c) -> p h c", h=2)[:, :, 0:quarter]
 
         q2 = [quantise(w2raw[z][:], "w2_%d" % z) for z in range(PASSES)]
-        for h, (lo, hi) in enumerate(((0, SHARED), (SHARED, T))):
+        for h, (lo, hi) in enumerate(pieces):
             gacc = ps.tile([P, hi - lo], F32, name="gacc%d" % lo)
             for z in range(PASSES):
                 product(gacc, q2[z], z, lo, hi)
-            nc.scalar.activation(out=keep[h], in_=gacc[:], func=ACT.Sigmoid, scale=-1.0)
-            nc.scalar.activation(out=gate[:, lo:hi], in_=gacc[:], func=ACT.Sigmoid)
+            if h == 0:
+                nc.scalar.activation(out=keep_first, in_=gacc[:].rearrange("p (h c) -> p h c", h=2), func=ACT.Sigmoid, scale=-1.0)
+            else:
+                nc.scalar.activation(out=keep_second[:], in_=gacc[:], func=ACT.Sigmoid, scale=-1.0)
+            nc.scalar.activation(out=gate[h], in_=gacc[:], func=ACT.Sigmoid)
 
         yacc = [ps.tile([P, hi - lo], F32, name="yacc%d" % lo) for lo, hi in pieces]
         for z in range(PASSES):
@@ -99,19 +100,12 @@ def tile_picked_wgmem_relu_l_kernel(tc, x_words, x_scales, mem, w1, w2, slot, ou
             for acc, (lo, hi) in zip(yacc, pieces):
                 product(acc, q1, z, lo, hi)
 
-        def make_fresh(i):
-            lo, hi = pieces[i]
-            nc.vector.scalar_tensor_tensor(out=fresh_at[i], in0=yacc[i][:], scalar=0.0, in1=gate[:, lo:hi], op0=ALU.max, op1=ALU.mult)
-
         nc.scalar.activation(out=old[:], in_=slots(SHARED, T), func=ACT.Copy)
-        nc.vector.tensor_tensor(kept_first, slots(0, FIRST), fresh[:, 0:FIRST], ALU.mult)
-        make_fresh(0)
-        nc.vector.tensor_tensor(kept[:, FIRST:SHARED], slots(FIRST, SHARED), fresh[:, FIRST:SHARED], ALU.mult)
-        nc.vector.tensor_tensor(new[:], kept_first, fresh_at[0], ALU.add)
-        nc.scalar.activation(out=slots(0, FIRST), in_=new[:], func=ACT.Copy)
-        make_fresh(1)
-        make_fresh(2)
-        nc.vector.tensor_tensor(kept[:, SHARED:T], old[:], keep_late[:], ALU.mult)
-        nc.vector.tensor_tensor(slots(FIRST, T), kept[:, FIRST:T], fresh[:, FIRST:T], ALU.add)
+        for i in range(2):
+            nc.vector.tensor_tensor(kept[:, i * quarter : (i + 1) * quarter], slots(i * quarter, (i + 1) * quarter), fresh[:, i * SHARED : i * SHARED + quarter], ALU.mult)
+        for h, (lo, hi) in enumerate(pieces):
+            nc.vector.scalar_tensor_tensor(out=fresh[:, lo:hi], in0=yacc[h][:], scalar=0.0, in1=gate[h], op0=ALU.max, op1=ALU.mult)
+        nc.vector.tensor_tensor(kept[:, SHARED:T], old[:], keep_second[:], ALU.mult)
+        nc.vector.tensor_tensor(slots(0, T), kept[:], fresh[:], ALU.add)
 
         nc.sync.dma_start(out=out, in_=window[:])

@@ -19,7 +19,7 @@ ACT = mybir.ActivationFunctionType
 P = 128
 PACK = 4
 PASSES = K // (P * PACK)
-SHARED = 256
+SHARED = 320
 
 
 def tile_picked_wgmem_relu_l_kernel(tc, x_words, x_scales, mem, w1, w2, slot, out):
@@ -73,39 +73,33 @@ def tile_picked_wgmem_relu_l_kernel(tc, x_words, x_scales, mem, w1, w2, slot, ou
         def slots(lo, hi):
             return window[:].indirect(offsets[:, lo // 16 : hi // 16])
 
-        pieces = ((0, SHARED), (SHARED, T))
+        halves = ((0, T // 2), (T // 2, T))
         kept = sb.tile([P, T], F32, name="kept")
-        fresh = sb.tile([P, T], F32, name="fresh")
+        gate = sb.tile([P, T], F32, name="gate")
         old = sb.tile([P, T - SHARED], F32, name="old")
-        gate_second = sb.tile([P, T - SHARED], F32, name="gate_second")
-        keep_second = sb.tile([P, T - SHARED], F32, name="keep_second")
-        gate = (kept[:, SHARED:T], gate_second[:])
-        quarter = SHARED // 2
-        keep_first = fresh[:].rearrange("p (h c) -> p h c", h=2)[:, :, 0:quarter]
+        terms = sb.tile([P, 2 * T - SHARED], F32, name="terms")
+        fresh = terms[:, 0:T]
+        keep = terms[:, T - SHARED : 2 * T - SHARED]
 
         q2 = [quantise(w2raw[z][:], "w2_%d" % z) for z in range(PASSES)]
-        for h, (lo, hi) in enumerate(pieces):
+        for lo, hi in halves:
             gacc = ps.tile([P, hi - lo], F32, name="gacc%d" % lo)
             for z in range(PASSES):
                 product(gacc, q2[z], z, lo, hi)
-            if h == 0:
-                nc.scalar.activation(out=keep_first, in_=gacc[:].rearrange("p (h c) -> p h c", h=2), func=ACT.Sigmoid, scale=-1.0)
-            else:
-                nc.scalar.activation(out=keep_second[:], in_=gacc[:], func=ACT.Sigmoid, scale=-1.0)
-            nc.scalar.activation(out=gate[h], in_=gacc[:], func=ACT.Sigmoid)
+            nc.scalar.activation(out=keep[:, lo:hi], in_=gacc[:], func=ACT.Sigmoid, scale=-1.0)
+            nc.scalar.activation(out=gate[:, lo:hi], in_=gacc[:], func=ACT.Sigmoid)
 
-        yacc = [ps.tile([P, hi - lo], F32, name="yacc%d" % lo) for lo, hi in pieces]
+        yacc = [ps.tile([P, hi - lo], F32, name="yacc%d" % lo) for lo, hi in halves]
         for z in range(PASSES):
             q1 = quantise(w1raw[z][:], "w1_%d" % z)
-            for acc, (lo, hi) in zip(yacc, pieces):
+            for acc, (lo, hi) in zip(yacc, halves):
                 product(acc, q1, z, lo, hi)
 
         nc.scalar.activation(out=old[:], in_=slots(SHARED, T), func=ACT.Copy)
-        for i in range(2):
-            nc.vector.tensor_tensor(kept[:, i * quarter : (i + 1) * quarter], slots(i * quarter, (i + 1) * quarter), fresh[:, i * SHARED : i * SHARED + quarter], ALU.mult)
-        for h, (lo, hi) in enumerate(pieces):
-            nc.vector.scalar_tensor_tensor(out=fresh[:, lo:hi], in0=yacc[h][:], scalar=0.0, in1=gate[h], op0=ALU.max, op1=ALU.mult)
-        nc.vector.tensor_tensor(kept[:, SHARED:T], old[:], keep_second[:], ALU.mult)
-        nc.vector.tensor_tensor(slots(0, T), kept[:], fresh[:], ALU.add)
+        nc.vector.tensor_tensor(kept[:, 0:SHARED], slots(0, SHARED), keep[:, 0:SHARED], ALU.mult)
+        nc.vector.tensor_tensor(kept[:, SHARED:T], old[:], keep[:, SHARED:T], ALU.mult)
+        for h, (lo, hi) in enumerate(halves):
+            nc.vector.scalar_tensor_tensor(out=fresh[:, lo:hi], in0=yacc[h][:], scalar=0.0, in1=gate[:, lo:hi], op0=ALU.max, op1=ALU.mult)
+        nc.vector.tensor_tensor(slots(0, T), kept[:], fresh, ALU.add)
 
         nc.sync.dma_start(out=out, in_=window[:])

@@ -74,20 +74,24 @@ def tile_picked_wgmem_relu_l_kernel(tc, x_words, x_scales, mem, w1, w2, slot, ou
             return window[:].indirect(offsets[:, lo // 16 : hi // 16])
 
         halves = ((0, T // 2), (T // 2, T))
+        middle = SHARED // 2
         kept = sb.tile([P, T], F32, name="kept")
         gate = sb.tile([P, T], F32, name="gate")
         old = sb.tile([P, T - SHARED], F32, name="old")
-        terms = sb.tile([P, 2 * T - SHARED], F32, name="terms")
-        fresh = terms[:, 0:T]
-        keep = terms[:, T - SHARED : 2 * T - SHARED]
+        keep_late = sb.tile([P, T - SHARED], F32, name="keep_late")
+        fresh = sb.tile([P, T], F32, name="fresh")
+        keep = fresh[:, T // 2 - middle : T // 2 + middle]
 
         q2 = [quantise(w2raw[z][:], "w2_%d" % z) for z in range(PASSES)]
-        for lo, hi in halves:
-            gacc = ps.tile([P, hi - lo], F32, name="gacc%d" % lo)
+        gacc = [ps.tile([P, hi - lo], F32, name="gacc%d" % lo) for lo, hi in halves]
+        for acc, (lo, hi) in zip(gacc, halves):
             for z in range(PASSES):
-                product(gacc, q2[z], z, lo, hi)
-            nc.scalar.activation(out=keep[:, lo:hi], in_=gacc[:], func=ACT.Sigmoid, scale=-1.0)
-            nc.scalar.activation(out=gate[:, lo:hi], in_=gacc[:], func=ACT.Sigmoid)
+                product(acc, q2[z], z, lo, hi)
+        nc.scalar.activation(out=keep[:, 0 : T // 2], in_=gacc[0][:], func=ACT.Sigmoid, scale=-1.0)
+        nc.scalar.activation(out=gate[:, 0 : T // 2], in_=gacc[0][:], func=ACT.Sigmoid)
+        nc.scalar.activation(out=keep[:, T // 2 : SHARED], in_=gacc[1][:, 0 : SHARED - T // 2], func=ACT.Sigmoid, scale=-1.0)
+        nc.scalar.activation(out=keep_late[:], in_=gacc[1][:, SHARED - T // 2 : T // 2], func=ACT.Sigmoid, scale=-1.0)
+        nc.scalar.activation(out=gate[:, T // 2 : T], in_=gacc[1][:], func=ACT.Sigmoid)
 
         yacc = [ps.tile([P, hi - lo], F32, name="yacc%d" % lo) for lo, hi in halves]
         for z in range(PASSES):
@@ -96,10 +100,11 @@ def tile_picked_wgmem_relu_l_kernel(tc, x_words, x_scales, mem, w1, w2, slot, ou
                 product(acc, q1, z, lo, hi)
 
         nc.scalar.activation(out=old[:], in_=slots(SHARED, T), func=ACT.Copy)
-        nc.vector.tensor_tensor(kept[:, 0:SHARED], slots(0, SHARED), keep[:, 0:SHARED], ALU.mult)
-        nc.vector.tensor_tensor(kept[:, SHARED:T], old[:], keep[:, SHARED:T], ALU.mult)
+        for lo, hi in ((0, middle), (middle, SHARED)):
+            nc.vector.tensor_tensor(kept[:, lo:hi], slots(lo, hi), keep[:, lo:hi], ALU.mult)
+        nc.gpsimd.tensor_tensor(kept[:, SHARED:T], old[:], keep_late[:], ALU.mult)
         for h, (lo, hi) in enumerate(halves):
             nc.vector.scalar_tensor_tensor(out=fresh[:, lo:hi], in0=yacc[h][:], scalar=0.0, in1=gate[:, lo:hi], op0=ALU.max, op1=ALU.mult)
-        nc.vector.tensor_tensor(slots(0, T), kept[:], fresh, ALU.add)
+        nc.vector.tensor_tensor(slots(0, T), kept[:], fresh[:], ALU.add)
 
         nc.sync.dma_start(out=out, in_=window[:])

@@ -19,7 +19,7 @@ ACT = mybir.ActivationFunctionType
 P = 128
 PACK = 4
 PASSES = K // (P * PACK)
-SHARED = 320
+SHARED = 256
 
 
 def tile_picked_wgmem_relu_l_kernel(tc, x_words, x_scales, mem, w1, w2, slot, out):
@@ -55,8 +55,11 @@ def tile_picked_wgmem_relu_l_kernel(tc, x_words, x_scales, mem, w1, w2, slot, ou
             grouped = sb.tile([P, N, PACK], BF16, name=name + "g", align_bytes=64)
             codes = sb.tile([P, N], U32, name=name + "c", align_bytes=64)
             scales = sb.tile([P, N], U8, name=name + "s", align_bytes=64)
-            nc.vector.tensor_copy(out=grouped[:], in_=raw.rearrange("p j m -> p m j"))
-            nc.vector.quantize_mx(out=codes[:].bitcast(FP8X4), scales=scales[:], in_=grouped[:].rearrange("p m j -> p (m j)"))
+            columns = (slice(0, N // 2), slice(N // 2, N))
+            for c in columns:
+                nc.vector.tensor_copy(out=grouped[:, c, :].rearrange("p (c i) j -> p c j i", i=PACK), in_=raw[:, :, c].rearrange("p j (c i) -> p c j i", i=PACK))
+            for c in columns:
+                nc.vector.quantize_mx(out=codes[:, c].bitcast(FP8X4), scales=scales[:, c], in_=grouped[:, c, :].rearrange("p m j -> p (m j)"))
             return codes, scales
 
         def product(acc, q, z, lo, hi):
@@ -89,7 +92,6 @@ def tile_picked_wgmem_relu_l_kernel(tc, x_words, x_scales, mem, w1, w2, slot, ou
                 product(acc, q2[z], z, lo, hi)
         nc.scalar.activation(out=keep[:, 0 : T // 2], in_=gacc[0][:], func=ACT.Sigmoid, scale=-1.0)
         nc.scalar.activation(out=gate[:, 0 : T // 2], in_=gacc[0][:], func=ACT.Sigmoid)
-        nc.scalar.activation(out=keep[:, T // 2 : SHARED], in_=gacc[1][:, 0 : SHARED - T // 2], func=ACT.Sigmoid, scale=-1.0)
         nc.scalar.activation(out=keep_late[:], in_=gacc[1][:, SHARED - T // 2 : T // 2], func=ACT.Sigmoid, scale=-1.0)
         nc.scalar.activation(out=gate[:, T // 2 : T], in_=gacc[1][:], func=ACT.Sigmoid)
 
@@ -99,10 +101,13 @@ def tile_picked_wgmem_relu_l_kernel(tc, x_words, x_scales, mem, w1, w2, slot, ou
             for acc, (lo, hi) in zip(yacc, halves):
                 product(acc, q1, z, lo, hi)
 
-        nc.scalar.activation(out=old[:], in_=slots(SHARED, T), func=ACT.Copy)
+        late = ((SHARED, (SHARED + T) // 2), ((SHARED + T) // 2, T))
+        for lo, hi in late:
+            nc.scalar.activation(out=old[:, lo - SHARED : hi - SHARED], in_=slots(lo, hi), func=ACT.Copy)
         for lo, hi in ((0, middle), (middle, SHARED)):
             nc.vector.tensor_tensor(kept[:, lo:hi], slots(lo, hi), keep[:, lo:hi], ALU.mult)
-        nc.gpsimd.tensor_tensor(kept[:, SHARED:T], old[:], keep_late[:], ALU.mult)
+        for lo, hi in late:
+            nc.gpsimd.tensor_tensor(kept[:, lo:hi], old[:, lo - SHARED : hi - SHARED], keep_late[:, lo - SHARED : hi - SHARED], ALU.mult)
         for h, (lo, hi) in enumerate(halves):
             nc.vector.scalar_tensor_tensor(out=fresh[:, lo:hi], in0=yacc[h][:], scalar=0.0, in1=gate[:, lo:hi], op0=ALU.max, op1=ALU.mult)
         nc.vector.tensor_tensor(slots(0, T), kept[:], fresh[:], ALU.add)

@@ -76,39 +76,38 @@ def tile_picked_wgmem_relu_l_kernel(tc, x_words, x_scales, mem, w1, w2, slot, ou
         def slots(lo, hi):
             return window[:].indirect(offsets[:, lo // 16 : hi // 16])
 
-        halves = ((0, T // 2), (T // 2, T))
-        middle = SHARED // 2
+        quarter = T // 4
+        pieces = ((0, quarter), (quarter, 2 * quarter), (2 * quarter, T))
         kept = sb.tile([P, T], F32, name="kept")
         gate = sb.tile([P, T], F32, name="gate")
         old = sb.tile([P, T - SHARED], F32, name="old")
         keep_late = sb.tile([P, T - SHARED], F32, name="keep_late")
         fresh = sb.tile([P, T], F32, name="fresh")
-        keep = fresh[:, T // 2 - middle : T // 2 + middle]
+        keep = (fresh[:, quarter // 2 : quarter // 2 + quarter], fresh[:, 2 * quarter : 3 * quarter], keep_late[:, 0:quarter], keep_late[:, quarter : 2 * quarter])
 
         q2 = [quantise(w2raw[z][:], "w2_%d" % z) for z in range(PASSES)]
-        gacc = [ps.tile([P, hi - lo], F32, name="gacc%d" % lo) for lo, hi in halves]
-        for acc, (lo, hi) in zip(gacc, halves):
+        for i in range(4):
+            lo, hi = i * quarter, (i + 1) * quarter
+            gacc = ps.tile([P, quarter], F32, name="gacc%d" % lo)
             for z in range(PASSES):
-                product(acc, q2[z], z, lo, hi)
-        nc.scalar.activation(out=keep[:, 0 : T // 2], in_=gacc[0][:], func=ACT.Sigmoid, scale=-1.0)
-        nc.scalar.activation(out=gate[:, 0 : T // 2], in_=gacc[0][:], func=ACT.Sigmoid)
-        nc.scalar.activation(out=keep_late[:], in_=gacc[1][:, SHARED - T // 2 : T // 2], func=ACT.Sigmoid, scale=-1.0)
-        nc.scalar.activation(out=gate[:, T // 2 : T], in_=gacc[1][:], func=ACT.Sigmoid)
+                product(gacc, q2[z], z, lo, hi)
+            nc.scalar.activation(out=keep[i], in_=gacc[:], func=ACT.Sigmoid, scale=-1.0)
+            nc.scalar.activation(out=gate[:, lo:hi], in_=gacc[:], func=ACT.Sigmoid)
 
-        yacc = [ps.tile([P, hi - lo], F32, name="yacc%d" % lo) for lo, hi in halves]
+        yacc = [ps.tile([P, hi - lo], F32, name="yacc%d" % lo) for lo, hi in pieces]
         for z in range(PASSES):
             q1 = quantise(w1raw[z][:], "w1_%d" % z)
-            for acc, (lo, hi) in zip(yacc, halves):
+            for acc, (lo, hi) in zip(yacc, pieces):
                 product(acc, q1, z, lo, hi)
 
         late = ((SHARED, (SHARED + T) // 2), ((SHARED + T) // 2, T))
         for lo, hi in late:
             nc.scalar.activation(out=old[:, lo - SHARED : hi - SHARED], in_=slots(lo, hi), func=ACT.Copy)
-        for lo, hi in ((0, middle), (middle, SHARED)):
-            nc.vector.tensor_tensor(kept[:, lo:hi], slots(lo, hi), keep[:, lo:hi], ALU.mult)
+        for i, (lo, hi) in enumerate(pieces[:2]):
+            nc.vector.tensor_tensor(kept[:, lo:hi], slots(lo, hi), keep[i], ALU.mult)
         for lo, hi in late:
             nc.gpsimd.tensor_tensor(kept[:, lo:hi], old[:, lo - SHARED : hi - SHARED], keep_late[:, lo - SHARED : hi - SHARED], ALU.mult)
-        for h, (lo, hi) in enumerate(halves):
+        for h, (lo, hi) in enumerate(pieces):
             nc.vector.scalar_tensor_tensor(out=fresh[:, lo:hi], in0=yacc[h][:], scalar=0.0, in1=gate[:, lo:hi], op0=ALU.max, op1=ALU.mult)
         nc.vector.tensor_tensor(slots(0, T), kept[:], fresh[:], ALU.add)
 

@@ -41,7 +41,7 @@ def tile_picked_wgmem_relu_l_kernel(tc, x_words, x_scales, mem, w1, w2, slot, ou
         for z in range(PASSES):
             load_weight(w2raw, w2, z)
         for q in range(4):
-            nc.sync.dma_start(
+            (nc.sync if q == 3 else nc.scalar).dma_start(
                 out=xs[32 * q : 32 * q + 4, :].bitcast(I32).rearrange("r (z c) -> r z c", z=PASSES),
                 in_=x_scales[:, 4 * q : 4 * q + 4, :].bitcast(I32).rearrange("z r c -> r z c"),
             )

@@ -38,13 +38,17 @@ def tile_picked_wgmem_relu_l_kernel(tc, x_words, x_scales, mem, w1, w2, slot, ou
         def load_weight(raw, w, z):
             nc.sync.dma_start(out=raw[z][:].rearrange("p j m -> p (j m)"), in_=w[z * P * PACK : (z + 1) * P * PACK, :].rearrange("(p j) m -> p (j m)", j=PACK))
 
-        for z in range(PASSES):
-            load_weight(w2raw, w2, z)
-        for q in range(4):
-            (nc.sync if q == 3 else nc.scalar).dma_start(
+        def load_scales(queue, q):
+            queue.dma_start(
                 out=xs[32 * q : 32 * q + 4, :].bitcast(I32).rearrange("r (z c) -> r z c", z=PASSES),
                 in_=x_scales[:, 4 * q : 4 * q + 4, :].bitcast(I32).rearrange("z r c -> r z c"),
             )
+
+        for q in range(3):
+            load_scales(nc.scalar, q)
+        load_weight(w2raw, w2, 0)
+        load_scales(nc.sync, 3)
+        load_weight(w2raw, w2, 1)
         nc.sync.dma_start(out=xw[:].bitcast(I32).rearrange("p (z c) -> p z c", z=PASSES), in_=x_words.bitcast(I32).rearrange("z p c -> p z c"))
         for z in range(PASSES):
             load_weight(w1raw, w1, z)

@@ -20,6 +20,7 @@ P = 128
 PACK = 4
 PASSES = K // (P * PACK)
 SHARED = 256
+ROW_ALIGN = 256
 
 
 def tile_picked_wgmem_relu_l_kernel(tc, x_words, x_scales, mem, w1, w2, slot, out):
@@ -29,11 +30,11 @@ def tile_picked_wgmem_relu_l_kernel(tc, x_words, x_scales, mem, w1, w2, slot, ou
         ps = ctx.enter_context(tc.psum_pool(name="ps", bufs=1))
 
         offsets = sb.tile([P, T // 16], U16, name="offsets")
-        window = sb.tile([P, U], F32, name="window")
-        xw = sb.tile([P, PASSES * 2 * T], U8, name="xw", align_bytes=64)
-        xs = sb.tile([P, PASSES * T], U8, name="xs", align_bytes=64)
-        w1raw = [sb.tile([P, PACK, N], F32, name="w1raw%d" % z) for z in range(PASSES)]
-        w2raw = [sb.tile([P, PACK, N], F32, name="w2raw%d" % z) for z in range(PASSES)]
+        window = sb.tile([P, U], F32, name="window", align_bytes=ROW_ALIGN)
+        xw = sb.tile([P, PASSES * 2 * T], U8, name="xw", align_bytes=ROW_ALIGN)
+        xs = sb.tile([P, PASSES * T], U8, name="xs", align_bytes=ROW_ALIGN)
+        w1raw = [sb.tile([P, PACK, N], F32, name="w1raw%d" % z, align_bytes=ROW_ALIGN) for z in range(PASSES)]
+        w2raw = [sb.tile([P, PACK, N], F32, name="w2raw%d" % z, align_bytes=ROW_ALIGN) for z in range(PASSES)]
 
         def load_weight(raw, w, z):
             nc.sync.dma_start(out=raw[z][:].rearrange("p j m -> p (j m)"), in_=w[z * P * PACK : (z + 1) * P * PACK, :].rearrange("(p j) m -> p (j m)", j=PACK))

@@ -29,7 +29,7 @@ def tile_picked_wgmem_relu_l_kernel(tc, x_words, x_scales, mem, w1, w2, slot, ou
         sb = ctx.enter_context(tc.tile_pool(name="sb", bufs=1))
         ps = ctx.enter_context(tc.psum_pool(name="ps", bufs=1))
 
-        offsets = sb.tile([P, T // 16], U16, name="offsets")
+        offsets = sb.tile([P, T // 16], U16, name="offsets", align_bytes=ROW_ALIGN)
         window = sb.tile([P, U], F32, name="window", align_bytes=ROW_ALIGN)
         xw = sb.tile([P, PASSES * 2 * T], U8, name="xw", align_bytes=ROW_ALIGN)
         xs = sb.tile([P, PASSES * T], U8, name="xs", align_bytes=ROW_ALIGN)
@@ -57,9 +57,9 @@ def tile_picked_wgmem_relu_l_kernel(tc, x_words, x_scales, mem, w1, w2, slot, ou
         nc.sync.dma_start(out=window[:], in_=mem)
 
         def quantise(raw, name):
-            grouped = sb.tile([P, N, PACK], BF16, name=name + "g", align_bytes=64)
-            codes = sb.tile([P, N], U32, name=name + "c", align_bytes=64)
-            scales = sb.tile([P, N], U8, name=name + "s", align_bytes=64)
+            grouped = sb.tile([P, N, PACK], BF16, name=name + "g", align_bytes=ROW_ALIGN)
+            codes = sb.tile([P, N], U32, name=name + "c", align_bytes=ROW_ALIGN)
+            scales = sb.tile([P, N], U8, name=name + "s", align_bytes=ROW_ALIGN)
             columns = (slice(0, N // 2), slice(N // 2, N))
             for c in columns:
                 nc.vector.tensor_copy(out=grouped[:, c, :].rearrange("p (c i) j -> p c j i", i=PACK), in_=raw[:, :, c].rearrange("p j (c i) -> p c j i", i=PACK))
@@ -83,11 +83,11 @@ def tile_picked_wgmem_relu_l_kernel(tc, x_words, x_scales, mem, w1, w2, slot, ou
 
         quarter = T // 4
         pieces = ((0, quarter), (quarter, 2 * quarter), (2 * quarter, T))
-        kept = sb.tile([P, T], F32, name="kept")
-        gate = sb.tile([P, T], F32, name="gate")
-        old = sb.tile([P, T - SHARED], F32, name="old")
-        keep_late = sb.tile([P, T - SHARED], F32, name="keep_late")
-        fresh = sb.tile([P, T], F32, name="fresh")
+        kept = sb.tile([P, T], F32, name="kept", align_bytes=ROW_ALIGN)
+        gate = sb.tile([P, T], F32, name="gate", align_bytes=ROW_ALIGN)
+        old = sb.tile([P, T - SHARED], F32, name="old", align_bytes=ROW_ALIGN)
+        keep_late = sb.tile([P, T - SHARED], F32, name="keep_late", align_bytes=ROW_ALIGN)
+        fresh = sb.tile([P, T], F32, name="fresh", align_bytes=ROW_ALIGN)
         keep = (fresh[:, quarter // 2 : quarter // 2 + quarter], fresh[:, 2 * quarter : 3 * quarter], keep_late[:, 0:quarter], keep_late[:, quarter : 2 * quarter])
 
         q2 = [quantise(w2raw[z][:], "w2_%d" % z) for z in range(PASSES)]

from contextlib import ExitStack

import concourse.mybir as mybir

K, T, N, U = 1024, 512, 128, 1024
FLOPS = 2 * 2 * K * T * N

F32 = mybir.dt.float32
BF16 = mybir.dt.bfloat16
I32 = mybir.dt.int32
U32 = mybir.dt.uint32
U16 = mybir.dt.uint16
U8 = mybir.dt.uint8
FP8X4 = mybir.dt.float8_e4m3fn_x4
FP4X4 = mybir.dt.float4_e2m1fn_x4
ALU = mybir.AluOpType
ACT = mybir.ActivationFunctionType

P = 128
PACK = 4
PASSES = K // (P * PACK)
SHARED = 256
ROW_ALIGN = 256


def tile_picked_wgmem_relu_l_kernel(tc, x_words, x_scales, mem, w1, w2, slot, out):
    nc = tc.nc
    with ExitStack() as ctx:
        sb = ctx.enter_context(tc.tile_pool(name="sb", bufs=1))
        ps = ctx.enter_context(tc.psum_pool(name="ps", bufs=1))

        offsets = sb.tile([P, T // 16], U16, name="offsets", align_bytes=ROW_ALIGN)
        window = sb.tile([P, U], F32, name="window", align_bytes=ROW_ALIGN)
        xw = sb.tile([P, PASSES * 2 * T], U8, name="xw", align_bytes=ROW_ALIGN)
        xs = sb.tile([P, PASSES * T], U8, name="xs", align_bytes=ROW_ALIGN)
        w1raw = [sb.tile([P, PACK, N], F32, name="w1raw%d" % z, align_bytes=ROW_ALIGN) for z in range(PASSES)]
        w2raw = [sb.tile([P, PACK, N], F32, name="w2raw%d" % z, align_bytes=ROW_ALIGN) for z in range(PASSES)]

        def load_weight(raw, w, z):
            nc.sync.dma_start(out=raw[z][:].rearrange("p j m -> p (j m)"), in_=w[z * P * PACK : (z + 1) * P * PACK, :].rearrange("(p j) m -> p (j m)", j=PACK))

        def load_scales(queue, q):
            queue.dma_start(
                out=xs[32 * q : 32 * q + 4, :].bitcast(I32).rearrange("r (z c) -> r z c", z=PASSES),
                in_=x_scales[:, 4 * q : 4 * q + 4, :].bitcast(I32).rearrange("z r c -> r z c"),
            )

        for q in range(3):
            load_scales(nc.scalar, q)
        load_weight(w2raw, w2, 0)
        load_scales(nc.sync, 3)
        load_weight(w2raw, w2, 1)
        nc.sync.dma_start(out=xw[:].bitcast(I32).rearrange("p (z c) -> p z c", z=PASSES), in_=x_words.bitcast(I32).rearrange("z p c -> p z c"))
        for z in range(PASSES):
            load_weight(w1raw, w1, z)
        nc.sync.dma_start(offsets[:], slot)
        nc.sync.dma_start(out=window[:], in_=mem)

        def quantise(raw, name):
            grouped = sb.tile([P, N, PACK], BF16, name=name + "g", align_bytes=ROW_ALIGN)
            codes = sb.tile([P, N], U32, name=name + "c", align_bytes=ROW_ALIGN)
            scales = sb.tile([P, N], U8, name=name + "s", align_bytes=ROW_ALIGN)
            columns = (slice(0, N // 2), slice(N // 2, N))
            for c in columns:
                nc.vector.tensor_copy(out=grouped[:, c, :].rearrange("p (c i) j -> p c j i", i=PACK), in_=raw[:, :, c].rearrange("p j (c i) -> p c j i", i=PACK))
            for c in columns:
                nc.vector.quantize_mx(out=codes[:, c].bitcast(FP8X4), scales=scales[:, c], in_=grouped[:, c, :].rearrange("p m j -> p (m j)"))
            return codes, scales

        def product(acc, q, z, lo, hi):
            nc.tensor.matmul_mx(
                out=acc[:],
                lhsT=q[0][:].bitcast(FP8X4),
                lhsT_scale=q[1][:],
                rhs=xw[:, 2 * (z * T + lo) : 2 * (z * T + hi)].bitcast(FP4X4),
                rhs_scale=xs[:, z * T + lo : z * T + hi],
                start=(z == 0),
                stop=(z == PASSES - 1),
            )

        def slots(lo, hi):
            return window[:].indirect(offsets[:, lo // 16 : hi // 16])

        quarter = T // 4
        pieces = ((0, quarter), (quarter, 2 * quarter), (2 * quarter, T))
        kept = sb.tile([P, T], F32, name="kept", align_bytes=ROW_ALIGN)
        gate = sb.tile([P, T], F32, name="gate", align_bytes=ROW_ALIGN)
        old = sb.tile([P, T - SHARED], F32, name="old", align_bytes=ROW_ALIGN)
        keep_late = sb.tile([P, T - SHARED], F32, name="keep_late", align_bytes=ROW_ALIGN)
        fresh = sb.tile([P, T], F32, name="fresh", align_bytes=ROW_ALIGN)
        keep = (fresh[:, quarter // 2 : quarter // 2 + quarter], fresh[:, 2 * quarter : 3 * quarter], keep_late[:, 0:quarter], keep_late[:, quarter : 2 * quarter])

        q2 = [quantise(w2raw[z][:], "w2_%d" % z) for z in range(PASSES)]
        for i in range(4):
            lo, hi = i * quarter, (i + 1) * quarter
            gacc = ps.tile([P, quarter], F32, name="gacc%d" % lo)
            for z in range(PASSES):
                product(gacc, q2[z], z, lo, hi)
            nc.scalar.activation(out=keep[i], in_=gacc[:], func=ACT.Sigmoid, scale=-1.0)
            nc.scalar.activation(out=gate[:, lo:hi], in_=gacc[:], func=ACT.Sigmoid)

        yacc = [ps.tile([P, hi - lo], F32, name="yacc%d" % lo) for lo, hi in pieces]
        for z in range(PASSES):
            q1 = quantise(w1raw[z][:], "w1_%d" % z)
            for acc, (lo, hi) in zip(yacc, pieces):
                product(acc, q1, z, lo, hi)

        late = ((SHARED, (SHARED + T) // 2), ((SHARED + T) // 2, T))
        for lo, hi in late:
            nc.scalar.activation(out=old[:, lo - SHARED : hi - SHARED], in_=slots(lo, hi), func=ACT.Copy)
        for i, (lo, hi) in enumerate(pieces[:2]):
            nc.vector.tensor_tensor(kept[:, lo:hi], slots(lo, hi), keep[i], ALU.mult)
        for lo, hi in late:
            nc.gpsimd.tensor_tensor(kept[:, lo:hi], old[:, lo - SHARED : hi - SHARED], keep_late[:, lo - SHARED : hi - SHARED], ALU.mult)
        for h, (lo, hi) in enumerate(pieces):
            nc.vector.scalar_tensor_tensor(out=fresh[:, lo:hi], in0=yacc[h][:], scalar=0.0, in1=gate[:, lo:hi], op0=ALU.max, op1=ALU.mult)
        nc.vector.tensor_tensor(slots(0, T), kept[:], fresh[:], ALU.add)

        nc.sync.dma_start(out=out, in_=window[:])
